import numpy as np
import ml_dtypes


def mxq(x, axis, fmt="e4m3"):
    dtype, down = {"e4m3": (ml_dtypes.float8_e4m3fn, 7), "e5m2": (ml_dtypes.float8_e5m2, 14)}[fmt]
    v = np.moveaxis(np.asarray(x, np.float32).astype(ml_dtypes.bfloat16).astype(np.float64), axis, -1)
    blocks = v.reshape(v.shape[:-1] + (-1, 32))
    amax = np.abs(blocks).max(-1, keepdims=True)
    byte = np.maximum(np.where(amax > 0, np.frexp(amax)[1] - 1 + 127, 0) - down, 1)
    scale = np.exp2(byte - 127.0)
    codes = (blocks / scale).astype(np.float32).astype(dtype).astype(np.float64)
    return np.moveaxis((codes * scale).reshape(v.shape), -1, axis)


WIDE = False


def mx_kscale(k):
    if not WIDE:
        return np.ones(k)
    levels = np.array([10, -10, 5, -5, 0])
    if k % 512:
        return np.exp2(np.random.permutation(np.resize(levels, k // 32))).repeat(32)
    a = np.empty((k // 512, 16))
    for p in range(k // 512):
        a[p, :8] = np.random.permutation(np.resize(levels, 8))
        for g in range(8):
            far = levels[np.abs(levels - a[p, g]) >= 10]
            a[p, g + 8] = far[np.random.randint(len(far))]
    return np.exp2(a.ravel()).repeat(32)


def f64(x):
    return np.asarray(x).astype(np.float64)


def striped(idx):
    return np.tile(idx.reshape(-1, 16).T, (8, 1)).astype(np.uint16)


def unstriped(offs):
    return offs[:16].T.reshape(-1).astype(np.int64)


def striped8(idx):
    return np.concatenate([x.reshape(-1, 16).T for x in idx]).astype(np.uint16)


def runs(offs, k):
    lists = np.stack([offs[16 * r : 16 * r + 16].T.reshape(-1) for r in range(8)]).astype(np.int64)
    return lists[np.arange(k) % 512 // 64]


def pack_weight(w):
    k, n = w.shape
    w = f64(np.asarray(w, np.float32).astype(ml_dtypes.bfloat16)).reshape(k // 32, 32, n)
    amax = np.abs(w).max(1)
    byte = np.clip(np.where(amax > 0, np.frexp(amax)[1] - 1 + 127 - 7, 1), 1, 254)
    scaled = (w * np.exp2(127.0 - byte)[:, None, :]).reshape(k, n).astype(np.float32)
    words = np.ascontiguousarray(scaled.reshape(k // 512, 128, 4, n).transpose(0, 1, 3, 2)).astype(ml_dtypes.float8_e4m3fn).view(np.uint8)
    return words, np.ascontiguousarray(byte.astype(np.uint8).reshape(k // 512, 16, n))


def unpack_weight(words, scales):
    g, p, n, _ = words.shape
    vals = np.ascontiguousarray(words).view(ml_dtypes.float8_e4m3fn).astype(np.float64) * np.repeat(np.exp2(scales.astype(np.float64) - 127.0), 8, axis=1)[..., None]
    return vals.transpose(0, 1, 3, 2).reshape(g * 512, n)


K, T, S, N, H, W = 512, 2048, 256, 512, 512, 128


def setup_inputs():
    n = np.random.standard_normal
    s = mx_kscale(K)[:, None]
    u = mx_kscale(H)
    packed_xT = pack_weight(n((K, T)) * s)
    perm = np.random.permutation(S)
    return {
        "x_words": packed_xT[0],
        "x_scales": packed_xT[1],
        "w1": (n((K, H)) / np.sqrt(K) / s).astype(np.float32),
        "gn": (np.random.uniform(0.5, 1.5, (H, 1)) * u[:, None]).astype(np.float32),
        "w2": (n((H, N)) / np.sqrt(2 * H) / u[:, None]).astype(np.float32),
        "w3": (n((K, N)) / np.sqrt(2 * K) / s).astype(np.float32),
        "offs": striped(np.random.permutation(T)[:S]),
        "n1": striped(perm[:W]),
        "n2": striped(perm[W:]),
        "two": striped(np.random.permutation(T)[:S]),
        "n3": striped8(np.stack([np.random.permutation(S) for _ in range(8)])),
    }


def reference(x_words, x_scales, w1, gn, w2, w3, offs, n1, n2, two, n3):
    xq = unpack_weight(x_words, x_scales)[:, unstriped(offs)]
    y = mxq(f64(w1), 0, "e4m3").T @ xq
    pa = y[:, unstriped(n1)]
    pb = y[:, unstriped(n2)]
    rb = np.maximum(0.5 * pa, pb)
    ra = pb - pa
    ds = np.zeros((H, S))
    ds[:, unstriped(n1)] = ra
    dt = ds.copy()
    dt[:, unstriped(n2)] = rb
    z = f64(gn) * dt
    x_two = unpack_weight(x_words, x_scales)[:, unstriped(two)]
    h = mxq(f64(w2), 0, "e4m3").T @ mxq(z, 0, "e4m3") + mxq(f64(w3), 0, "e4m3").T @ x_two
    pa2 = h[np.arange(N)[:, None], runs(n3, N)]
    return (2.0 * (h * pa2)) / ((h) ** 2 + (pa2) ** 2 + 0.5)

@@ -1,0 +1,197 @@
+from contextlib import ExitStack
+
+import concourse.mybir as mybir
+
+K, T, S, N, H, W = 512, 2048, 256, 512, 512, 128
+FLOPS = 2 * S * (K * H + H * N + K * N)
+
+F32 = mybir.dt.float32
+BF16 = mybir.dt.bfloat16
+I32 = mybir.dt.int32
+U32 = mybir.dt.uint32
+U16 = mybir.dt.uint16
+U8 = mybir.dt.uint8
+FP8X4 = mybir.dt.float8_e4m3fn_x4
+ALU = mybir.AluOpType
+ACT = mybir.ActivationFunctionType
+
+P = 128
+PACK = 4
+HALF = 256
+
+
+def tile_picked_mixinliftharm_none_p_kernel(
+    tc, x_words, x_scales, w1, gn, w2, w3, offs, n1, n2, two, n3, out
+):
+    nc = tc.nc
+    with ExitStack() as ctx:
+        lists = ctx.enter_context(tc.tile_pool(name="lists", bufs=1))
+        sb = ctx.enter_context(tc.tile_pool(name="sb", bufs=1))
+        psum = ctx.enter_context(tc.psum_pool(name="psum", bufs=1))
+
+        def load_list(src, name):
+            tile = lists.tile(list(src.shape), U16, name=name)
+            nc.sync.dma_start(tile[:], src)
+            return tile
+
+        def load_weight_half(w, half, name):
+            raw = sb.tile([P, PACK, HALF], F32, name=name)
+            cols = slice(half * HALF, (half + 1) * HALF)
+            nc.sync.dma_start(raw[:], w.rearrange("(p j) c -> p j c", j=PACK)[:, :, cols])
+            return raw
+
+        def round_and_deal(raw, half, grouped):
+            ms = slice(half * HALF // PACK, (half + 1) * HALF // PACK)
+            nc.vector.tensor_copy(
+                grouped[:, :, ms, :].rearrange("p t m j -> p m j t"),
+                raw[:].rearrange("p j (m t) -> p m j t", t=PACK),
+            )
+
+        def quantise(grouped, width, name):
+            codes = sb.tile([P, width], U32, name=name + "_codes", tag=name + "_codes", align_bytes=64)
+            scales = sb.tile([P, width], U8, name=name + "_scales", align_bytes=64)
+            nc.vector.quantize_mx(out=codes[:].bitcast(FP8X4), scales=scales[:], in_=grouped)
+            return codes, scales
+
+        def product(acc, w_q, t, x_q, start, stop):
+            cols = slice(t * P, (t + 1) * P)
+            nc.tensor.matmul_mx(
+                out=acc[:],
+                lhsT=w_q[0][:, cols].bitcast(FP8X4),
+                lhsT_scale=w_q[1][:, cols],
+                rhs=x_q[0][:].bitcast(FP8X4),
+                rhs_scale=x_q[1][:],
+                start=start,
+                stop=stop,
+            )
+
+        table_scales = sb.tile([P, T], U8, name="table_scales")
+        nc.vector.memset(table_scales[:].bitcast(I32), 0)
+        for q in range(4):
+            nc.scalar.dma_start(
+                table_scales[32 * q : 32 * q + 4, :].bitcast(I32), x_scales[0, 4 * q : 4 * q + 4, :].bitcast(I32)
+            )
+        offs_t = load_list(offs, "offs")
+        two_t = load_list(two, "two")
+        w1_raw = sb.tile([P, PACK, H], F32, name="w1_raw")
+        nc.sync.dma_start(w1_raw[:], w1.rearrange("(p j) c -> p j c", j=PACK))
+        table_words = sb.tile([P, T], I32, name="table_words")
+        nc.sync.dma_start(table_words[:], x_words[0].rearrange("p c r -> p (c r)").bitcast(I32))
+        n1_t = load_list(n1, "n1")
+        n2_t = load_list(n2, "n2")
+        w3_raw = [load_weight_half(w3, half, f"w3_raw{half}") for half in range(2)]
+        w2_raw = [load_weight_half(w2, half, f"w2_raw{half}") for half in range(2)]
+        gain = sb.tile([P, PACK], F32, name="gain")
+        nc.sync.dma_start(gain[:], gn.rearrange("(p t) o -> p (t o)", t=PACK))
+        n3_t = load_list(n3, "n3")
+
+        def pick_scales(idx, name, tag):
+            picked = sb.tile([P, S], U8, name=name, tag=tag, align_bytes=64)
+            nc.vector.tensor_copy(picked[:], table_scales[:].indirect(idx[:]))
+            return picked
+
+        def pick_words(idx, name):
+            picked = sb.tile([P, S], U32, name=name, align_bytes=64)
+            nc.vector.tensor_copy(picked[:], table_words[:].bitcast(U32).indirect(idx[:]))
+            return picked
+
+        def quantise_weight(raw, name, tag):
+            grouped = sb.tile([P, PACK, P, PACK], BF16, name=name + "_grouped", tag=tag, align_bytes=64)
+            for half in range(2):
+                round_and_deal(raw[half], half, grouped)
+            return quantise(grouped[:].rearrange("p t m j -> p (t m j)"), PACK * P, name)
+
+        w1_src = w1_raw[:].rearrange("p j (m t) -> p m j t", t=PACK)
+        w1_q = []
+        for pair, copy in enumerate((nc.vector.tensor_copy, nc.scalar.copy)):
+            grouped = sb.tile([P, 2, P, PACK], BF16, name=f"w1_grouped{pair}", tag=f"w1_grouped{pair}", align_bytes=64)
+            copy(grouped[:].rearrange("p t m j -> p m j t"), w1_src[:, :, :, 2 * pair : 2 * pair + 2])
+            w1_q.append(quantise(grouped[:].rearrange("p t m j -> p (t m j)"), 2 * P, f"w1_{pair}"))
+            if pair == 0:
+                x1_scales = pick_scales(offs_t, "x1_scales", "w1_grouped0")
+        x1_q = (pick_words(offs_t, "x1_words"), x1_scales)
+
+        x2_words = pick_words(two_t, "x2_words")
+
+        def evacuate(dst, acc, t):
+            if t == 0:
+                nc.scalar.copy(dst[:], acc[:])
+            else:
+                nc.vector.tensor_copy(dst[:], acc[:])
+
+        y = []
+        for t in range(PACK):
+            acc = psum.tile([P, S], F32, name=f"y_acc{t}")
+            product(acc, w1_q[t // 2], t % 2, x1_q, True, True)
+            y_t = sb.tile([P, S], F32, name=f"y{t}")
+            evacuate(y_t, acc, t)
+            y.append(y_t)
+
+        pa = sb.tile([P, PACK, W], F32, name="pa")
+        pb = sb.tile([P, PACK, W], F32, name="pb")
+        ra = sb.tile([P, PACK, W], F32, name="ra")
+        rb = sb.tile([P, PACK, W], F32, name="rb")
+        for pair in range(2):
+            ts = slice(2 * pair, 2 * pair + 2)
+            for t in range(ts.start, ts.stop):
+                nc.scalar.activation(pa[:, t, :], y[t][:].indirect(n1_t[:]), ACT.Copy)
+                nc.scalar.activation(pb[:, t, :], y[t][:].indirect(n2_t[:]), ACT.Copy)
+            nc.vector.tensor_tensor(ra[:, ts, :], pb[:, ts, :], pa[:, ts, :], ALU.subtract)
+            nc.vector.scalar_tensor_tensor(rb[:, ts, :], pa[:, ts, :], 0.5, pb[:, ts, :], ALU.mult, ALU.max)
+
+        x2_q = (x2_words, pick_scales(two_t, "x2_scales", "w1_0_codes"))
+        w3_q = quantise_weight(w3_raw, "w3", "w1_1_codes")
+        h_acc = [psum.tile([P, S], F32, name=f"h_acc{t}") for t in range(PACK)]
+        for t in range(PACK):
+            product(h_acc[t], w3_q, t, x2_q, True, False)
+        w2_q = quantise_weight(w2_raw, "w2", "g2")
+
+        dt = [sb.tile([P, S], F32, name=f"dt{t}") for t in range(PACK)]
+        z = sb.tile([P, S, PACK], BF16, name="z", tag="g2", align_bytes=64)
+        for pair in range(2):
+            for src, idx in ((ra, n1_t), (rb, n2_t)):
+                for t in (2 * pair, 2 * pair + 1):
+                    nc.scalar.activation(dt[t][:].indirect(idx[:]), src[:, t, :], ACT.Copy)
+            for t in (2 * pair, 2 * pair + 1):
+                nc.vector.tensor_scalar(z[:, :, t], dt[t][:], gain[:, t : t + 1], None, ALU.mult)
+        z_q = quantise(z[:].rearrange("p s t -> p (s t)"), S, "z")
+        for t in range(PACK):
+            product(h_acc[t], w2_q, t, z_q, False, True)
+
+        out_rows = out.rearrange("(p t) s -> p t s", t=PACK)
+        def tiles(name):
+            return [sb.tile([P, S], F32, name=f"{name}{t}") for t in range(PACK)]
+
+        h, pa2, hh, pp, num, den, root, inv, res = [
+            tiles(name) for name in ("h", "pa2", "hh", "pp", "num", "den", "root", "inv", "res")
+        ]
+
+        def square(dst, src, on_scalar):
+            if on_scalar:
+                nc.scalar.activation(dst[:], src[:], ACT.Square)
+            else:
+                nc.vector.tensor_tensor(dst[:], src[:], src[:], ALU.mult)
+
+        for t in range(PACK):
+            evacuate(h[t], h_acc[t], t)
+        for t in range(PACK):
+            for half in range(2):
+                nc.scalar.activation(
+                    pa2[t][:, half * W : (half + 1) * W],
+                    h[t][:].indirect(n3_t[:, half * 8 : (half + 1) * 8]),
+                    ACT.Copy,
+                )
+            square(hh[t], h[t], t >= 2)
+        for t in range(PACK):
+            square(pp[t], pa2[t], t == 3)
+            nc.vector.scalar_tensor_tensor(num[t][:], h[t][:], 2.0, pa2[t][:], ALU.mult, ALU.mult)
+            nc.vector.scalar_tensor_tensor(den[t][:], pp[t][:], 0.5, hh[t][:], ALU.add, ALU.add)
+        for pair in range(2):
+            ts = (2 * pair, 2 * pair + 1)
+            for t in ts:
+                nc.scalar.activation(root[t][:], den[t][:], ACT.Abs_reciprocal_sqrt)
+            for t in ts:
+                nc.scalar.activation(inv[t][:], root[t][:], ACT.Square)
+            for t in ts:
+                nc.vector.tensor_tensor(res[t][:], num[t][:], inv[t][:], ALU.mult)
+                nc.sync.dma_start(out_rows[:, t, :], res[t][:])

@@ -34,18 +34,10 @@ def tile_picked_mixinliftharm_none_p_kernel(
             nc.sync.dma_start(tile[:], src)
             return tile
 
-        def load_weight_half(w, half, name):
-            raw = sb.tile([P, PACK, HALF], F32, name=name)
-            cols = slice(half * HALF, (half + 1) * HALF)
+        def load_weight(w, cols, name):
+            raw = sb.tile([P, PACK, cols.stop - cols.start], F32, name=name)
             nc.sync.dma_start(raw[:], w.rearrange("(p j) c -> p j c", j=PACK)[:, :, cols])
-            return raw
-
-        def round_and_deal(raw, half, grouped):
-            ms = slice(half * HALF // PACK, (half + 1) * HALF // PACK)
-            nc.vector.tensor_copy(
-                grouped[:, :, ms, :].rearrange("p t m j -> p m j t"),
-                raw[:].rearrange("p j (m t) -> p m j t", t=PACK),
-            )
+            return raw[:].rearrange("p j (m t) -> p m t j", t=PACK)
 
         def quantise(grouped, width, name):
             codes = sb.tile([P, width], U32, name=name + "_codes", tag=name + "_codes", align_bytes=64)
@@ -56,7 +48,7 @@ def tile_picked_mixinliftharm_none_p_kernel(
         def product(acc, w_q, t, x_q, start, stop):
             cols = slice(t * P, (t + 1) * P)
             nc.tensor.matmul_mx(
-                out=acc[:],
+                out=acc,
                 lhsT=w_q[0][:, cols].bitcast(FP8X4),
                 lhsT_scale=w_q[1][:, cols],
                 rhs=x_q[0][:].bitcast(FP8X4),
@@ -71,16 +63,18 @@ def tile_picked_mixinliftharm_none_p_kernel(
             nc.scalar.dma_start(
                 table_scales[32 * q : 32 * q + 4, :].bitcast(I32), x_scales[0, 4 * q : 4 * q + 4, :].bitcast(I32)
             )
+        warm = sb.tile([P, 16], F32, name="warm")
+        nc.vector.memset(warm[:, 0:1], 1.0)
+        nc.scalar.activation(warm[:, 8:9], warm[:, 0:1], ACT.Abs_reciprocal_sqrt)
         offs_t = load_list(offs, "offs")
         two_t = load_list(two, "two")
-        w1_raw = sb.tile([P, PACK, H], F32, name="w1_raw")
-        nc.sync.dma_start(w1_raw[:], w1.rearrange("(p j) c -> p j c", j=PACK))
-        table_words = sb.tile([P, T], I32, name="table_words")
+        table_words = sb.tile([P, T], I32, name="table_words", tag="table_words", align_bytes=64)
         nc.sync.dma_start(table_words[:], x_words[0].rearrange("p c r -> p (c r)").bitcast(I32))
+        w1_raw = [load_weight(w1, cols, f"w1_raw{cols.start}") for cols in (slice(0, HALF), slice(HALF, H))]
         n1_t = load_list(n1, "n1")
         n2_t = load_list(n2, "n2")
-        w3_raw = [load_weight_half(w3, half, f"w3_raw{half}") for half in range(2)]
-        w2_raw = [load_weight_half(w2, half, f"w2_raw{half}") for half in range(2)]
+        w3_raw = load_weight(w3, slice(0, N), "w3_raw")
+        w2_raw = load_weight(w2, slice(0, N), "w2_raw")
         gain = sb.tile([P, PACK], F32, name="gain")
         nc.sync.dma_start(gain[:], gn.rearrange("(p t) o -> p (t o)", t=PACK))
         n3_t = load_list(n3, "n3")
@@ -95,55 +89,61 @@ def tile_picked_mixinliftharm_none_p_kernel(
             nc.vector.tensor_copy(picked[:], table_words[:].bitcast(U32).indirect(idx[:]))
             return picked
 
+        m_halves = (slice(0, P // 2), slice(P // 2, P))
+
         def quantise_weight(raw, name, tag):
             grouped = sb.tile([P, PACK, P, PACK], BF16, name=name + "_grouped", tag=tag, align_bytes=64)
-            for half in range(2):
-                round_and_deal(raw[half], half, grouped)
+            for ms in m_halves:
+                nc.vector.tensor_copy(grouped[:].rearrange("p t m j -> p m t j")[:, ms], raw[:, ms])
             return quantise(grouped[:].rearrange("p t m j -> p (t m j)"), PACK * P, name)
 
-        w1_src = w1_raw[:].rearrange("p j (m t) -> p m j t", t=PACK)
-        w1_q = []
-        for pair, copy in enumerate((nc.vector.tensor_copy, nc.scalar.copy)):
-            grouped = sb.tile([P, 2, P, PACK], BF16, name=f"w1_grouped{pair}", tag=f"w1_grouped{pair}", align_bytes=64)
-            copy(grouped[:].rearrange("p t m j -> p m j t"), w1_src[:, :, :, 2 * pair : 2 * pair + 2])
-            w1_q.append(quantise(grouped[:].rearrange("p t m j -> p (t m j)"), 2 * P, f"w1_{pair}"))
-            if pair == 0:
-                x1_scales = pick_scales(offs_t, "x1_scales", "w1_grouped0")
-        x1_q = (pick_words(offs_t, "x1_words"), x1_scales)
-
+        x1_words = pick_words(offs_t, "x1_words")
         x2_words = pick_words(two_t, "x2_words")
+        x1_q = (x1_words, pick_scales(offs_t, "x1_scales", "table_words"))
+
+        lo = sb.tile([P, 2, P, PACK], BF16, name="w1_lo", align_bytes=64)
+        hi = sb.tile([P, 2, P, PACK], BF16, name="w1_hi", tag="w1_hi", align_bytes=64)
+        lo_dst = lo[:].rearrange("p t m j -> p m t j")
+        hi_dst = hi[:].rearrange("p t m j -> p m t j")
+        nc.vector.tensor_copy(lo_dst[:, m_halves[0]], w1_raw[0][:, :, 0:2, :])
+        for half in range(2):
+            nc.scalar.copy(hi_dst[:, m_halves[half]], w1_raw[half][:, :, 2:4, :])
+        for t in range(2):
+            nc.vector.tensor_copy(lo[:, t, m_halves[1], :], w1_raw[1][:, :, t, :])
+        w1_q = [quantise(lo[:, t].rearrange("p m j -> p (m j)"), P, f"w1_{t}") for t in range(2)]
+        w1_q.append(quantise(hi[:].rearrange("p t m j -> p (t m j)"), 2 * P, "w1_hi"))
+        x2_q = (x2_words, pick_scales(two_t, "x2_scales", "w1_hi"))
 
         def evacuate(dst, acc, t):
             if t == 0:
-                nc.scalar.copy(dst[:], acc[:])
+                nc.scalar.copy(dst, acc[:])
             else:
-                nc.vector.tensor_copy(dst[:], acc[:])
+                nc.vector.tensor_copy(dst, acc[:])
 
         y = []
         for t in range(PACK):
             acc = psum.tile([P, S], F32, name=f"y_acc{t}")
-            product(acc, w1_q[t // 2], t % 2, x1_q, True, True)
+            product(acc[:], w1_q[min(t, 2)], max(t - 2, 0), x1_q, True, True)
             y_t = sb.tile([P, S], F32, name=f"y{t}")
-            evacuate(y_t, acc, t)
+            evacuate(y_t[:], acc, t)
             y.append(y_t)
 
         pa = sb.tile([P, PACK, W], F32, name="pa")
         pb = sb.tile([P, PACK, W], F32, name="pb")
-        ra = sb.tile([P, PACK, W], F32, name="ra")
-        rb = sb.tile([P, PACK, W], F32, name="rb")
-        for pair in range(2):
-            ts = slice(2 * pair, 2 * pair + 2)
-            for t in range(ts.start, ts.stop):
-                nc.scalar.activation(pa[:, t, :], y[t][:].indirect(n1_t[:]), ACT.Copy)
-                nc.scalar.activation(pb[:, t, :], y[t][:].indirect(n2_t[:]), ACT.Copy)
-            nc.vector.tensor_tensor(ra[:, ts, :], pb[:, ts, :], pa[:, ts, :], ALU.subtract)
-            nc.vector.scalar_tensor_tensor(rb[:, ts, :], pa[:, ts, :], 0.5, pb[:, ts, :], ALU.mult, ALU.max)
+        window = [sb.tile([P, 2 * S], F32, name=f"window{t}") for t in range(PACK)]
+        h = [window[t][:, :S] for t in range(PACK)]
+        ra = [window[t][:, S : S + W] for t in range(PACK)]
+        rb = [window[t][:, S + W :] for t in range(PACK)]
+        for t in range(PACK):
+            nc.scalar.activation(pa[:, t, :], y[t][:].indirect(n1_t[:]), ACT.Copy)
+            nc.scalar.activation(pb[:, t, :], y[t][:].indirect(n2_t[:]), ACT.Copy)
+            nc.vector.tensor_tensor(ra[t], pb[:, t, :], pa[:, t, :], ALU.subtract)
+            nc.vector.scalar_tensor_tensor(rb[t], pa[:, t, :], 0.5, pb[:, t, :], ALU.mult, ALU.max)
 
-        x2_q = (x2_words, pick_scales(two_t, "x2_scales", "w1_0_codes"))
-        w3_q = quantise_weight(w3_raw, "w3", "w1_1_codes")
+        w3_q = quantise_weight(w3_raw, "w3", "w1_hi_codes")
         h_acc = [psum.tile([P, S], F32, name=f"h_acc{t}") for t in range(PACK)]
         for t in range(PACK):
-            product(h_acc[t], w3_q, t, x2_q, True, False)
+            product(h_acc[t][:], w3_q, t, x2_q, True, False)
         w2_q = quantise_weight(w2_raw, "w2", "g2")
 
         dt = [sb.tile([P, S], F32, name=f"dt{t}") for t in range(PACK)]
@@ -151,47 +151,48 @@ def tile_picked_mixinliftharm_none_p_kernel(
         for pair in range(2):
             for src, idx in ((ra, n1_t), (rb, n2_t)):
                 for t in (2 * pair, 2 * pair + 1):
-                    nc.scalar.activation(dt[t][:].indirect(idx[:]), src[:, t, :], ACT.Copy)
-            for t in (2 * pair, 2 * pair + 1):
-                nc.vector.tensor_scalar(z[:, :, t], dt[t][:], gain[:, t : t + 1], None, ALU.mult)
-        z_q = quantise(z[:].rearrange("p s t -> p (s t)"), S, "z")
-        for t in range(PACK):
-            product(h_acc[t], w2_q, t, z_q, False, True)
+                    nc.scalar.activation(dt[t][:].indirect(idx[:]), src[t], ACT.Copy)
+        halves = (slice(0, W), slice(W, S))
+        for t in range(PACK - 1):
+            nc.vector.tensor_scalar(z[:, :, t], dt[t][:], gain[:, t : t + 1], None, ALU.mult)
+        for cols in halves:
+            nc.vector.tensor_scalar(z[:, cols, PACK - 1], dt[PACK - 1][:, cols], gain[:, PACK - 1 :], None, ALU.mult)
+        z_q = [quantise(z[:, cols, :].rearrange("p s t -> p (s t)"), W, f"z{cols.start}") for cols in halves]
+        for half, cols in enumerate(halves):
+            for t in range(PACK):
+                product(h_acc[t][:, cols], w2_q, t, z_q[half], False, half == 1)
 
         out_rows = out.rearrange("(p t) s -> p t s", t=PACK)
-        def tiles(name):
-            return [sb.tile([P, S], F32, name=f"{name}{t}") for t in range(PACK)]
-
-        h, pa2, hh, pp, num, den, root, inv, res = [
-            tiles(name) for name in ("h", "pa2", "hh", "pp", "num", "den", "root", "inv", "res")
+        pa2, hh, pp, num, den, root, inv, res = [
+            sb.tile([P, PACK, S], F32, name=name) for name in ("pa2", "hh", "pp", "num", "den", "root", "inv", "res")
         ]
 
         def square(dst, src, on_scalar):
             if on_scalar:
-                nc.scalar.activation(dst[:], src[:], ACT.Square)
+                nc.scalar.activation(dst, src, ACT.Square)
             else:
-                nc.vector.tensor_tensor(dst[:], src[:], src[:], ALU.mult)
+                nc.vector.tensor_tensor(dst, src, src, ALU.mult)
 
         for t in range(PACK):
             evacuate(h[t], h_acc[t], t)
         for t in range(PACK):
-            for half in range(2):
-                nc.scalar.activation(
-                    pa2[t][:, half * W : (half + 1) * W],
-                    h[t][:].indirect(n3_t[:, half * 8 : (half + 1) * 8]),
-                    ACT.Copy,
-                )
-            square(hh[t], h[t], t >= 2)
+            nc.scalar.activation(pa2[:, t, :], window[t][:].indirect(n3_t[:]), ACT.Copy)
         for t in range(PACK):
-            square(pp[t], pa2[t], t == 3)
-            nc.vector.scalar_tensor_tensor(num[t][:], h[t][:], 2.0, pa2[t][:], ALU.mult, ALU.mult)
-            nc.vector.scalar_tensor_tensor(den[t][:], pp[t][:], 0.5, hh[t][:], ALU.add, ALU.add)
-        for pair in range(2):
-            ts = (2 * pair, 2 * pair + 1)
-            for t in ts:
-                nc.scalar.activation(root[t][:], den[t][:], ACT.Abs_reciprocal_sqrt)
-            for t in ts:
-                nc.scalar.activation(inv[t][:], root[t][:], ACT.Square)
-            for t in ts:
-                nc.vector.tensor_tensor(res[t][:], num[t][:], inv[t][:], ALU.mult)
-                nc.sync.dma_start(out_rows[:, t, :], res[t][:])
+            square(hh[:, t, :], h[t], t >= 2)
+        for step in range(PACK + 1):
+            if step < PACK:
+                square(pp[:, step, :], pa2[:, step, :], False)
+            if step > 0:
+                t = step - 1
+                nc.vector.scalar_tensor_tensor(den[:, t, :], pp[:, t, :], 0.5, hh[:, t, :], ALU.add, ALU.add)
+        for t in range(PACK):
+            nc.vector.scalar_tensor_tensor(num[:, t, :], h[t], 2.0, pa2[:, t, :], ALU.mult, ALU.mult)
+        for step in range(PACK + 1):
+            if step < PACK:
+                nc.scalar.activation(root[:, step, :], den[:, step, :], ACT.Abs_reciprocal_sqrt)
+            if step > 0:
+                t = step - 1
+                nc.scalar.activation(inv[:, t, :], root[:, t, :], ACT.Square)
+        for t in range(PACK):
+            nc.vector.tensor_tensor(res[:, t, :], num[:, t, :], inv[:, t, :], ALU.mult)
+            nc.sync.dma_start(out_rows[:, t, :], res[:, t, :])

from contextlib import ExitStack

import concourse.mybir as mybir

K, T, S, N, H, W = 512, 2048, 256, 512, 512, 128
FLOPS = 2 * S * (K * H + H * N + K * N)

F32 = mybir.dt.float32
BF16 = mybir.dt.bfloat16
I32 = mybir.dt.int32
U32 = mybir.dt.uint32
U16 = mybir.dt.uint16
U8 = mybir.dt.uint8
FP8X4 = mybir.dt.float8_e4m3fn_x4
ALU = mybir.AluOpType
ACT = mybir.ActivationFunctionType

P = 128
PACK = 4
HALF = 256


def tile_picked_mixinliftharm_none_p_kernel(
    tc, x_words, x_scales, w1, gn, w2, w3, offs, n1, n2, two, n3, out
):
    nc = tc.nc
    with ExitStack() as ctx:
        lists = ctx.enter_context(tc.tile_pool(name="lists", bufs=1))
        sb = ctx.enter_context(tc.tile_pool(name="sb", bufs=1))
        psum = ctx.enter_context(tc.psum_pool(name="psum", bufs=1))

        def load_list(src, name):
            tile = lists.tile(list(src.shape), U16, name=name)
            nc.sync.dma_start(tile[:], src)
            return tile

        def load_weight(w, cols, name):
            raw = sb.tile([P, PACK, cols.stop - cols.start], F32, name=name)
            nc.sync.dma_start(raw[:], w.rearrange("(p j) c -> p j c", j=PACK)[:, :, cols])
            return raw[:].rearrange("p j (m t) -> p m t j", t=PACK)

        def quantise(grouped, width, name):
            codes = sb.tile([P, width], U32, name=name + "_codes", tag=name + "_codes", align_bytes=64)
            scales = sb.tile([P, width], U8, name=name + "_scales", align_bytes=64)
            nc.vector.quantize_mx(out=codes[:].bitcast(FP8X4), scales=scales[:], in_=grouped)
            return codes, scales

        def product(acc, w_q, t, x_q, start, stop):
            cols = slice(t * P, (t + 1) * P)
            nc.tensor.matmul_mx(
                out=acc,
                lhsT=w_q[0][:, cols].bitcast(FP8X4),
                lhsT_scale=w_q[1][:, cols],
                rhs=x_q[0][:].bitcast(FP8X4),
                rhs_scale=x_q[1][:],
                start=start,
                stop=stop,
            )

        table_scales = sb.tile([P, T], U8, name="table_scales")
        nc.vector.memset(table_scales[:].bitcast(I32), 0)
        for q in range(4):
            nc.scalar.dma_start(
                table_scales[32 * q : 32 * q + 4, :].bitcast(I32), x_scales[0, 4 * q : 4 * q + 4, :].bitcast(I32)
            )
        warm = sb.tile([P, 16], F32, name="warm")
        nc.vector.memset(warm[:, 0:1], 1.0)
        nc.scalar.activation(warm[:, 8:9], warm[:, 0:1], ACT.Abs_reciprocal_sqrt)
        offs_t = load_list(offs, "offs")
        two_t = load_list(two, "two")
        table_words = sb.tile([P, T], I32, name="table_words", tag="table_words", align_bytes=64)
        nc.sync.dma_start(table_words[:], x_words[0].rearrange("p c r -> p (c r)").bitcast(I32))
        w1_raw = [load_weight(w1, cols, f"w1_raw{cols.start}") for cols in (slice(0, HALF), slice(HALF, H))]
        n1_t = load_list(n1, "n1")
        n2_t = load_list(n2, "n2")
        w3_raw = load_weight(w3, slice(0, N), "w3_raw")
        w2_raw = load_weight(w2, slice(0, N), "w2_raw")
        gain = sb.tile([P, PACK], F32, name="gain")
        nc.sync.dma_start(gain[:], gn.rearrange("(p t) o -> p (t o)", t=PACK))
        n3_t = load_list(n3, "n3")

        def pick_scales(idx, name, tag):
            picked = sb.tile([P, S], U8, name=name, tag=tag, align_bytes=64)
            nc.vector.tensor_copy(picked[:], table_scales[:].indirect(idx[:]))
            return picked

        def pick_words(idx, name):
            picked = sb.tile([P, S], U32, name=name, align_bytes=64)
            nc.vector.tensor_copy(picked[:], table_words[:].bitcast(U32).indirect(idx[:]))
            return picked

        m_halves = (slice(0, P // 2), slice(P // 2, P))

        def quantise_weight(raw, name, tag):
            grouped = sb.tile([P, PACK, P, PACK], BF16, name=name + "_grouped", tag=tag, align_bytes=64)
            for ms in m_halves:
                nc.vector.tensor_copy(grouped[:].rearrange("p t m j -> p m t j")[:, ms], raw[:, ms])
            return quantise(grouped[:].rearrange("p t m j -> p (t m j)"), PACK * P, name)

        x1_words = pick_words(offs_t, "x1_words")
        x2_words = pick_words(two_t, "x2_words")
        x1_q = (x1_words, pick_scales(offs_t, "x1_scales", "table_words"))

        lo = sb.tile([P, 2, P, PACK], BF16, name="w1_lo", align_bytes=64)
        hi = sb.tile([P, 2, P, PACK], BF16, name="w1_hi", tag="w1_hi", align_bytes=64)
        lo_dst = lo[:].rearrange("p t m j -> p m t j")
        hi_dst = hi[:].rearrange("p t m j -> p m t j")
        nc.vector.tensor_copy(lo_dst[:, m_halves[0]], w1_raw[0][:, :, 0:2, :])
        for half in range(2):
            nc.scalar.copy(hi_dst[:, m_halves[half]], w1_raw[half][:, :, 2:4, :])
        for t in range(2):
            nc.vector.tensor_copy(lo[:, t, m_halves[1], :], w1_raw[1][:, :, t, :])
        w1_q = [quantise(lo[:, t].rearrange("p m j -> p (m j)"), P, f"w1_{t}") for t in range(2)]
        w1_q.append(quantise(hi[:].rearrange("p t m j -> p (t m j)"), 2 * P, "w1_hi"))
        x2_q = (x2_words, pick_scales(two_t, "x2_scales", "w1_hi"))

        def evacuate(dst, acc, t):
            if t == 0:
                nc.scalar.copy(dst, acc[:])
            else:
                nc.vector.tensor_copy(dst, acc[:])

        y = []
        for t in range(PACK):
            acc = psum.tile([P, S], F32, name=f"y_acc{t}")
            product(acc[:], w1_q[min(t, 2)], max(t - 2, 0), x1_q, True, True)
            y_t = sb.tile([P, S], F32, name=f"y{t}")
            evacuate(y_t[:], acc, t)
            y.append(y_t)

        pa = sb.tile([P, PACK, W], F32, name="pa")
        pb = sb.tile([P, PACK, W], F32, name="pb")
        window = [sb.tile([P, 2 * S], F32, name=f"window{t}") for t in range(PACK)]
        h = [window[t][:, :S] for t in range(PACK)]
        ra = [window[t][:, S : S + W] for t in range(PACK)]
        rb = [window[t][:, S + W :] for t in range(PACK)]
        for t in range(PACK):
            nc.scalar.activation(pa[:, t, :], y[t][:].indirect(n1_t[:]), ACT.Copy)
            nc.scalar.activation(pb[:, t, :], y[t][:].indirect(n2_t[:]), ACT.Copy)
            nc.vector.tensor_tensor(ra[t], pb[:, t, :], pa[:, t, :], ALU.subtract)
            nc.vector.scalar_tensor_tensor(rb[t], pa[:, t, :], 0.5, pb[:, t, :], ALU.mult, ALU.max)

        w3_q = quantise_weight(w3_raw, "w3", "w1_hi_codes")
        h_acc = [psum.tile([P, S], F32, name=f"h_acc{t}") for t in range(PACK)]
        for t in range(PACK):
            product(h_acc[t][:], w3_q, t, x2_q, True, False)
        w2_q = quantise_weight(w2_raw, "w2", "g2")

        dt = [sb.tile([P, S], F32, name=f"dt{t}") for t in range(PACK)]
        z = sb.tile([P, S, PACK], BF16, name="z", tag="g2", align_bytes=64)
        for pair in range(2):
            for src, idx in ((ra, n1_t), (rb, n2_t)):
                for t in (2 * pair, 2 * pair + 1):
                    nc.scalar.activation(dt[t][:].indirect(idx[:]), src[t], ACT.Copy)
        halves = (slice(0, W), slice(W, S))
        for t in range(PACK - 1):
            nc.vector.tensor_scalar(z[:, :, t], dt[t][:], gain[:, t : t + 1], None, ALU.mult)
        for cols in halves:
            nc.vector.tensor_scalar(z[:, cols, PACK - 1], dt[PACK - 1][:, cols], gain[:, PACK - 1 :], None, ALU.mult)
        z_q = [quantise(z[:, cols, :].rearrange("p s t -> p (s t)"), W, f"z{cols.start}") for cols in halves]
        for half, cols in enumerate(halves):
            for t in range(PACK):
                product(h_acc[t][:, cols], w2_q, t, z_q[half], False, half == 1)

        out_rows = out.rearrange("(p t) s -> p t s", t=PACK)
        pa2, hh, pp, num, den, root, inv, res = [
            sb.tile([P, PACK, S], F32, name=name) for name in ("pa2", "hh", "pp", "num", "den", "root", "inv", "res")
        ]

        def square(dst, src, on_scalar):
            if on_scalar:
                nc.scalar.activation(dst, src, ACT.Square)
            else:
                nc.vector.tensor_tensor(dst, src, src, ALU.mult)

        for t in range(PACK):
            evacuate(h[t], h_acc[t], t)
        for t in range(PACK):
            nc.scalar.activation(pa2[:, t, :], window[t][:].indirect(n3_t[:]), ACT.Copy)
        for t in range(PACK):
            square(hh[:, t, :], h[t], t >= 2)
        for step in range(PACK + 1):
            if step < PACK:
                square(pp[:, step, :], pa2[:, step, :], False)
            if step > 0:
                t = step - 1
                nc.vector.scalar_tensor_tensor(den[:, t, :], pp[:, t, :], 0.5, hh[:, t, :], ALU.add, ALU.add)
        for t in range(PACK):
            nc.vector.scalar_tensor_tensor(num[:, t, :], h[t], 2.0, pa2[:, t, :], ALU.mult, ALU.mult)
        for step in range(PACK + 1):
            if step < PACK:
                nc.scalar.activation(root[:, step, :], den[:, step, :], ACT.Abs_reciprocal_sqrt)
            if step > 0:
                t = step - 1
                nc.scalar.activation(inv[:, t, :], root[:, t, :], ACT.Square)
        for t in range(PACK):
            nc.vector.tensor_tensor(res[:, t, :], num[:, t, :], inv[:, t, :], ALU.mult)
            nc.sync.dma_start(out_rows[:, t, :], res[:, t, :])
